import numpy as np
import ml_dtypes


def mxq(x, axis, fmt="e4m3"):
    dtype, down = {"e4m3": (ml_dtypes.float8_e4m3fn, 7), "e5m2": (ml_dtypes.float8_e5m2, 14)}[fmt]
    v = np.moveaxis(np.asarray(x, np.float32).astype(ml_dtypes.bfloat16).astype(np.float64), axis, -1)
    blocks = v.reshape(v.shape[:-1] + (-1, 32))
    amax = np.abs(blocks).max(-1, keepdims=True)
    byte = np.maximum(np.where(amax > 0, np.frexp(amax)[1] - 1 + 127, 0) - down, 1)
    scale = np.exp2(byte - 127.0)
    codes = (blocks / scale).astype(np.float32).astype(dtype).astype(np.float64)
    return np.moveaxis((codes * scale).reshape(v.shape), -1, axis)


WIDE = False


def mx_kscale(k):
    if not WIDE:
        return np.ones(k)
    levels = np.array([30, -30])
    if k % 512:
        return np.exp2(np.random.permutation(np.resize(levels, k // 32))).repeat(32)
    a = np.empty((k // 512, 16))
    for p in range(k // 512):
        a[p, :8] = np.random.permutation(np.resize(levels, 8))
        for g in range(8):
            far = levels[np.abs(levels - a[p, g]) >= 10]
            a[p, g + 8] = far[np.random.randint(len(far))]
    return np.exp2(a.ravel()).repeat(32)


def f64(x):
    return np.asarray(x).astype(np.float64)


def striped(idx):
    return np.tile(np.asarray(idx).reshape(-1, 16).T, (8, 1)).astype(np.uint16)


def unstriped(offs):
    return offs[:16].T.reshape(-1).astype(np.int64)


E2M1 = np.array([0.0, 0.5, 1.0, 1.5, 2.0, 3.0, 4.0, 6.0, -0.0, -0.5, -1.0, -1.5, -2.0, -3.0, -4.0, -6.0])


def pack_weight(w, fmt):
    k, n = w.shape
    w = f64(np.asarray(w, np.float32).astype(ml_dtypes.bfloat16)).reshape(k // 32, 32, n)
    amax = np.abs(w).max(1)
    if fmt in ("e4m3", "e5m2"):
        byte = np.frexp(amax)[1] - 1 + 127 - (7 if fmt == "e4m3" else 14)
    else:
        mant, ex = np.frexp(amax / 6.0)
        byte = np.where(mant > 0.5, ex, ex - 1) + 127
    byte = np.clip(np.where(amax > 0, byte, 1), 1, 254)
    scaled = (w * np.exp2(127.0 - byte)[:, None, :]).reshape(k, n).astype(np.float32)
    by_word = np.ascontiguousarray(scaled.reshape(k // 512, 128, 4, n).transpose(0, 1, 3, 2))
    if fmt in ("e4m3", "e5m2"):
        words = by_word.astype(ml_dtypes.float8_e4m3fn if fmt == "e4m3" else ml_dtypes.float8_e5m2).view(np.uint8)
    else:
        c = by_word.astype(ml_dtypes.float4_e2m1fn).view(np.uint8) & 0xF
        words = (c[..., 0::2] | (c[..., 1::2] << 4)).reshape(k // 512, 128, 2 * n)
    return np.ascontiguousarray(words), np.ascontiguousarray(byte.astype(np.uint8).reshape(k // 512, 16, n))


def unpack_weight(words, scales, fmt):
    g, _, n = scales.shape
    words = np.ascontiguousarray(words).reshape(g, 128, n, -1)
    if fmt in ("e4m3", "e5m2"):
        vals = words.view(ml_dtypes.float8_e4m3fn if fmt == "e4m3" else ml_dtypes.float8_e5m2).astype(np.float64)
    else:
        nib = np.empty((g, 128, n, 4), np.uint8)
        nib[..., 0::2] = words & 0xF
        nib[..., 1::2] = words >> 4
        vals = E2M1[nib]
    vals = vals * np.repeat(np.exp2(scales.astype(np.float64) - 127.0), 8, axis=1)[..., None]
    return vals.transpose(0, 1, 3, 2).reshape(g * 512, n)


def bf(x):
    return np.asarray(x, np.float32).astype(ml_dtypes.bfloat16)


def planes(Y):
    r, m = Y.shape
    b = f64(bf(Y)).reshape(r // 32, 32, m)
    amax = np.abs(b).max(1)
    byte = np.clip(np.where(amax > 0, np.frexp(amax)[1] - 1 + 127 - 7, 1), 1, 254)
    codes = (b * np.exp2(127.0 - byte)[:, None, :]).reshape(r, m).astype(np.float32).astype(ml_dtypes.float8_e4m3fn).view(np.uint8)
    words = codes.reshape(r // 512, 128, 4, m).transpose(0, 1, 3, 2)
    return np.ascontiguousarray(words), np.ascontiguousarray(byte.astype(np.uint8).reshape(r // 512, 16, m))


K, T, J, S, R, O, N = 1024, 512, 256, 512, 512, 128, 512


def setup_inputs():
    n = np.random.standard_normal
    idx = np.random.permutation(T)[:J]
    idx2 = np.random.permutation(S)[:J]
    idx3 = np.random.permutation(J)[:O]
    fk = mx_kscale(K)
    fr = mx_kscale(R)
    wp = pack_weight(n((K, R)) * 1 / np.sqrt(K) * fk[:, None] * fr, "e2m1")
    wbp = pack_weight(n((R, N)) * 1 / np.sqrt(R) / fr[:, None], "e5m2")
    return {
        "xa": (n((K, T))).astype(np.float32),
        "xb": (n((K, S))).astype(np.float32),
        "fk": (np.random.uniform(0.5, 2.0, (K, 1)) / fk[:, None]).astype(np.float32),
        "w_words": wp[0],
        "w_scales": wp[1],
        "wb_words": wbp[0],
        "wb_scales": wbp[1],
        "rs": (n((N, O))).astype(np.float32),
        "gm": (np.random.uniform(0.5, 2.0, (N, 1))).astype(np.float32),
        "offs": striped(idx),
        "offs2": striped(idx2),
        "offs3": striped(idx3),
    }


def reference(xa, xb, fk, w_words, w_scales, wb_words, wb_scales, rs, gm, offs, offs2, offs3):
    idx = unstriped(offs)
    idx2 = unstriped(offs2)
    idx3 = unstriped(offs3)
    wu = unpack_weight(w_words, w_scales, "e2m1")
    wbu = unpack_weight(wb_words, wb_scales, "e5m2")
    u = f64(xa)[:, idx] * f64(xb)[:, idx2] * f64(fk)
    uq = mxq(u, 0, "e4m3")
    a = wu.T @ uq
    ha = np.maximum(a, 0.0)
    hid = ha[:, idx3]
    hidq = mxq(hid, 0, "e5m2")
    p = wbu.T @ hidq
    y = f64(gm) * p + f64(rs)
    words, scales = planes(y)
    return y, words, scales

@@ -1,0 +1,194 @@
+from contextlib import ExitStack
+
+import concourse.mybir as mybir
+
+K, T, J, S, R, O, N = 1024, 512, 256, 512, 512, 128, 512
+FLOPS = 2 * K * R * J + 2 * R * N * O
+
+F32 = mybir.dt.float32
+BF16 = mybir.dt.bfloat16
+I32 = mybir.dt.int32
+U32 = mybir.dt.uint32
+U16 = mybir.dt.uint16
+U8 = mybir.dt.uint8
+E4M3X4 = mybir.dt.float8_e4m3fn_x4
+E5M2X4 = mybir.dt.float8_e5m2_x4
+E2M1X4 = mybir.dt.float4_e2m1fn_x4
+ALU = mybir.AluOpType
+ACT = mybir.ActivationFunctionType
+
+P = 128
+PACK = 4
+PASSES = K // (P * PACK)
+
+
+def interleave(nc, dst, src):
+    nc.vector.tensor_copy(
+        out=dst.rearrange("p (c i) t -> p c t i", i=4),
+        in_=src.rearrange("p t (c i) -> p c t i", i=4),
+    )
+
+
+def tile_list_entryproducts_relooked_residual_pl_kernel(
+    tc, xa, xb, fk, w_words, w_scales, wb_words, wb_scales, rs, gm, offs, offs2, offs3, out_0, out_1, out_2
+):
+    nc = tc.nc
+    with ExitStack() as ctx:
+        sb = ctx.enter_context(tc.tile_pool(name="sb", bufs=1))
+        psum = ctx.enter_context(tc.psum_pool(name="psum", bufs=1))
+
+        def tile(name, shape, dtype):
+            return sb.tile(shape, dtype, name=name, align_bytes=64)
+
+        list_a = tile("list_a", [P, J // 16], U16)
+        list_b = tile("list_b", [P, J // 16], U16)
+        list_h = tile("list_h", [P, O // 16], U16)
+        fk_sb = tile("fk_sb", [P, PASSES, PACK], F32)
+        gm_sb = tile("gm_sb", [P, PACK], F32)
+        rs_sb = tile("rs_sb", [P, PACK, O], F32)
+        w_raw = tile("w_raw", [P, PASSES * 2 * R], U8)
+        ws_raw = tile("ws_raw", [P, PASSES * R], U8)
+        wb_raw = tile("wb_raw", [P, N], I32)
+        wbs_raw = tile("wbs_raw", [P, N], U8)
+        xa_sb = [tile("xa%d" % g, [P, T], F32) for g in range(PASSES * PACK)]
+        xb_sb = [tile("xb%d" % g, [P, 2 * S], F32) for g in range(PASSES * PACK // 2)]
+
+        nc.gpsimd.memset(ws_raw[:].bitcast(I32), 0)
+        nc.gpsimd.memset(wbs_raw[:].bitcast(I32), 0)
+
+        xa_rows = xa.rearrange("(z p i) t -> z i p t", p=P, i=PACK)
+        xb_rows = xb.rearrange("(z p h e) s -> z h p (e s)", p=P, h=2, e=2)
+
+        def load_a(g):
+            nc.sync.dma_start(out=xa_sb[g][:], in_=xa_rows[g // PACK, g % PACK])
+
+        def load_b(h):
+            nc.sync.dma_start(out=xb_sb[h][:], in_=xb_rows[h // 2, h % 2])
+
+        def load_ws(q):
+            nc.sync.dma_start(
+                out=ws_raw[32 * q : 32 * q + 4, :].bitcast(I32).rearrange("p (z c) -> p z c", z=PASSES),
+                in_=w_scales[:, 4 * q : 4 * q + 4, :].rearrange("z r c -> r z c").bitcast(I32),
+            )
+
+        def load_wbs(q):
+            nc.sync.dma_start(
+                out=wbs_raw[32 * q : 32 * q + 4, :].bitcast(I32),
+                in_=wb_scales[0, 4 * q : 4 * q + 4, :].bitcast(I32),
+            )
+
+        nc.sync.dma_start(list_b[:], offs2)
+        load_b(0)
+        nc.sync.dma_start(out=fk_sb[:], in_=fk.rearrange("(z p i) o -> p z (i o)", p=P, i=PACK))
+        nc.sync.dma_start(
+            out=w_raw[:].bitcast(I32).rearrange("p (z c) -> p z c", z=PASSES),
+            in_=w_words.rearrange("z p c -> p z c").bitcast(I32),
+        )
+        nc.sync.dma_start(list_a[:], offs)
+        load_a(0)
+        load_ws(0)
+        load_b(1)
+        load_ws(1)
+        load_a(1)
+        load_ws(2)
+        load_a(2)
+        load_ws(3)
+        load_b(2)
+        nc.sync.dma_start(list_h[:], offs3)
+        load_a(3)
+        load_wbs(0)
+        load_a(4)
+        load_wbs(1)
+        load_b(3)
+        load_wbs(2)
+        load_a(5)
+        load_wbs(3)
+        load_a(6)
+        load_a(7)
+        nc.sync.dma_start(out=wb_raw[:], in_=wb_words[0].rearrange("p n t -> p (n t)").bitcast(I32))
+        nc.sync.dma_start(out=gm_sb[:], in_=gm.rearrange("(p t) o -> p (t o)", t=PACK))
+        nc.sync.dma_start(out=rs_sb[:], in_=rs.rearrange("(p t) o -> p t o", t=PACK))
+
+        w_sb = tile("w_sb", [P, PASSES * 2 * R], U8)
+        ws_sb = tile("ws_sb", [P, PASSES * R], U8)
+        wb_sb = tile("wb_sb", [P, N], I32)
+        wbs_sb = tile("wbs_sb", [P, N], U8)
+
+        def deal(dst, src, z):
+            nc.vector.tensor_copy(
+                out=dst.rearrange("p (z t m) -> p z t m", z=z, t=PACK),
+                in_=src.rearrange("p (z m t) -> p z t m", z=z, t=PACK),
+            )
+
+        acc1 = [psum.tile([P, J], F32, name="acc1_%d" % t) for t in range(PACK)]
+        for z in range(PASSES):
+            prod = tile("prod%d" % z, [P, PACK, J], F32)
+            for i in range(PACK):
+                g = z * PACK + i
+                gb = tile("gb%d" % g, [P, J], F32)
+                window = xb_sb[g // 2][:, (g % 2) * S : (g % 2 + 1) * S]
+                gb_raw = tile("gb_raw%d" % g, [P, J], F32)
+                nc.scalar.activation(gb_raw[:], window.indirect(list_b[:]), ACT.Copy)
+                nc.scalar.activation(gb[:], gb_raw[:], ACT.Copy, scale=fk_sb[:, z, i : i + 1])
+                nc.vector.tensor_tensor(prod[:, i, :], xa_sb[g][:].indirect(list_a[:]), gb[:], ALU.mult)
+                if g == 0:
+                    deal(w_sb[:].bitcast(U16), w_raw[:].bitcast(U16), PASSES)
+                if g == 2:
+                    deal(ws_sb[:], ws_raw[:], PASSES)
+            u_bf = tile("u_bf%d" % z, [P, J, PACK], BF16)
+            u_q = tile("u_q%d" % z, [P, J], U32)
+            u_s = tile("u_s%d" % z, [P, J], U8)
+            interleave(nc, u_bf[:], prod[:])
+            nc.vector.quantize_mx(out=u_q[:].bitcast(E4M3X4), scales=u_s[:], in_=u_bf[:].rearrange("p j t -> p (j t)"))
+            for t in range(PACK):
+                c = (z * PACK + t) * P
+                nc.tensor.matmul_mx(
+                    out=acc1[t][:],
+                    lhsT=w_sb[:, 2 * c : 2 * (c + P)].bitcast(E2M1X4),
+                    lhsT_scale=ws_sb[:, c : c + P],
+                    rhs=u_q[:].bitcast(E4M3X4),
+                    rhs_scale=u_s[:],
+                    start=(z == 0),
+                    stop=(z == PASSES - 1),
+                )
+
+        deal(wbs_sb[:], wbs_raw[:], 1)
+        deal(wb_sb[:], wb_raw[:], 1)
+
+        hid_bf = tile("hid_bf", [P, O, PACK], BF16)
+        for t in range(PACK):
+            ha = tile("ha%d" % t, [P, J], F32)
+            nc.scalar.activation(ha[:], acc1[t][:], ACT.Relu)
+            nc.vector.tensor_copy(hid_bf[:, :, t], ha[:].indirect(list_h[:]))
+        hid_q = tile("hid_q", [P, O], U32)
+        hid_s = tile("hid_s", [P, O], U8)
+        nc.vector.quantize_mx(out=hid_q[:].bitcast(E5M2X4), scales=hid_s[:], in_=hid_bf[:].rearrange("p o t -> p (o t)"))
+
+        y = tile("y", [P, PACK, O], F32)
+        for t in range(PACK):
+            acc2 = psum.tile([P, O], F32, name="acc2_%d" % t)
+            nc.tensor.matmul_mx(
+                out=acc2[:],
+                lhsT=wb_sb[:, t * P : (t + 1) * P].bitcast(E5M2X4),
+                lhsT_scale=wbs_sb[:, t * P : (t + 1) * P],
+                rhs=hid_q[:].bitcast(E5M2X4),
+                rhs_scale=hid_s[:],
+                start=True,
+                stop=True,
+            )
+            nc.vector.scalar_tensor_tensor(
+                out=y[:, t, :], in0=acc2[:], scalar=gm_sb[:, t : t + 1], in1=rs_sb[:, t, :], op0=ALU.mult, op1=ALU.add
+            )
+        nc.sync.dma_start(out=out_0.rearrange("(p t) o -> p t o", t=PACK), in_=y[:])
+
+        y_bf = tile("y_bf", [P, O, PACK], BF16)
+        y_q = tile("y_q", [P, O], U32)
+        y_s = tile("y_s", [P, O], U8)
+        interleave(nc, y_bf[:], y[:])
+        nc.vector.quantize_mx(out=y_q[:].bitcast(E4M3X4), scales=y_s[:], in_=y_bf[:].rearrange("p o t -> p (o t)"))
+        nc.sync.dma_start(out=out_1[0].rearrange("p o t -> p (o t)").bitcast(I32), in_=y_q[:].bitcast(I32))
+        for q in range(4):
+            queue = nc.sync if q % 2 == 0 else nc.scalar
+            queue.dma_start(
+                out=out_2[0, 4 * q : 4 * q + 4, :].bitcast(I32), in_=y_s[32 * q : 32 * q + 4, :].bitcast(I32)
+            )

@@ -50,20 +50,33 @@ def tile_list_entryproducts_relooked_residual_pl_kernel(
         ws_raw = tile("ws_raw", [P, PASSES * R], U8)
         wb_raw = tile("wb_raw", [P, N], I32)
         wbs_raw = tile("wbs_raw", [P, N], U8)
-        xa_sb = [tile("xa%d" % g, [P, T], F32) for g in range(PASSES * PACK)]
-        xb_sb = [tile("xb%d" % g, [P, 2 * S], F32) for g in range(PASSES * PACK // 2)]
+        a_groups = [(0, 1), (2, 3), (4, 5), (6,), (7,)]
+        b_groups = [(0,), (1, 2), (3,), (4,), (5, 6), (7,)]
+        xa_t = [tile("xa%d" % gs[0], [P, len(gs) * T], F32) for gs in a_groups]
+        xb_t = [tile("xb%d" % gs[0], [P, len(gs) * S], F32) for gs in b_groups]
+        xa_whole = {gs[0]: xa_t[k][:] for k, gs in enumerate(a_groups)}
+        xb_whole = {gs[0]: xb_t[k][:] for k, gs in enumerate(b_groups)}
+        xa_sb = [xa_t[k][:, e * T : (e + 1) * T] for k, gs in enumerate(a_groups) for e in range(len(gs))]
+        xb_sb = [xb_t[k][:, e * S : (e + 1) * S] for k, gs in enumerate(b_groups) for e in range(len(gs))]
 
-        nc.gpsimd.memset(ws_raw[:].bitcast(I32), 0)
-        nc.gpsimd.memset(wbs_raw[:].bitcast(I32), 0)
+        warm_in = tile("warm_in", [P, 1], F32)
+        warm_out = tile("warm_out", [P, 1], F32)
+        nc.vector.memset(warm_in[:], 0.0)
+        nc.scalar.activation(warm_out[:], warm_in[:], ACT.Copy)
+        nc.vector.memset(ws_raw[:].bitcast(I32), 0)
+        nc.vector.memset(wbs_raw[:].bitcast(I32), 0)
 
-        xa_rows = xa.rearrange("(z p i) t -> z i p t", p=P, i=PACK)
-        xb_rows = xb.rearrange("(z p h e) s -> z h p (e s)", p=P, h=2, e=2)
+        def load_planes(dst, table, gs):
+            rows = table.rearrange("(z p i) c -> z p (i c)", p=P, i=PACK)
+            width = table.shape[1]
+            i = gs[0] % PACK
+            nc.sync.dma_start(out=dst[:], in_=rows[gs[0] // PACK, :, i * width : (i + len(gs)) * width])
 
-        def load_a(g):
-            nc.sync.dma_start(out=xa_sb[g][:], in_=xa_rows[g // PACK, g % PACK])
+        def load_a(k):
+            load_planes(xa_t[k], xa, a_groups[k])
 
-        def load_b(h):
-            nc.sync.dma_start(out=xb_sb[h][:], in_=xb_rows[h // 2, h % 2])
+        def load_b(k):
+            load_planes(xb_t[k], xb, b_groups[k])
 
         def load_ws(q):
             nc.sync.dma_start(
@@ -77,42 +90,37 @@ def tile_list_entryproducts_relooked_residual_pl_kernel(
                 in_=wb_scales[0, 4 * q : 4 * q + 4, :].bitcast(I32),
             )
 
-        nc.sync.dma_start(list_b[:], offs2)
-        load_b(0)
-        nc.sync.dma_start(out=fk_sb[:], in_=fk.rearrange("(z p i) o -> p z (i o)", p=P, i=PACK))
         nc.sync.dma_start(
             out=w_raw[:].bitcast(I32).rearrange("p (z c) -> p z c", z=PASSES),
             in_=w_words.rearrange("z p c -> p z c").bitcast(I32),
         )
+        nc.sync.dma_start(list_b[:], offs2)
+        load_b(0)
+        nc.sync.dma_start(out=fk_sb[:], in_=fk.rearrange("(z p i) o -> p z (i o)", p=P, i=PACK))
         nc.sync.dma_start(list_a[:], offs)
         load_a(0)
         load_ws(0)
         load_b(1)
         load_ws(1)
-        load_a(1)
         load_ws(2)
-        load_a(2)
         load_ws(3)
+        load_a(1)
         load_b(2)
-        nc.sync.dma_start(list_h[:], offs3)
-        load_a(3)
-        load_wbs(0)
-        load_a(4)
-        load_wbs(1)
         load_b(3)
-        load_wbs(2)
-        load_a(5)
-        load_wbs(3)
-        load_a(6)
-        load_a(7)
+        load_a(2)
+        load_b(4)
+        load_a(4)
+        load_a(3)
+        load_b(5)
         nc.sync.dma_start(out=wb_raw[:], in_=wb_words[0].rearrange("p n t -> p (n t)").bitcast(I32))
+        for q in range(4):
+            load_wbs(q)
+        nc.sync.dma_start(list_h[:], offs3)
         nc.sync.dma_start(out=gm_sb[:], in_=gm.rearrange("(p t) o -> p (t o)", t=PACK))
         nc.sync.dma_start(out=rs_sb[:], in_=rs.rearrange("(p t) o -> p t o", t=PACK))
 
         w_sb = tile("w_sb", [P, PASSES * 2 * R], U8)
         ws_sb = tile("ws_sb", [P, PASSES * R], U8)
-        wb_sb = tile("wb_sb", [P, N], I32)
-        wbs_sb = tile("wbs_sb", [P, N], U8)
 
         def deal(dst, src, z):
             nc.vector.tensor_copy(
@@ -120,26 +128,60 @@ def tile_list_entryproducts_relooked_residual_pl_kernel(
                 in_=src.rearrange("p (z m t) -> p z t m", z=z, t=PACK),
             )
 
+        deal(w_sb[:].bitcast(U16), w_raw[:].bitcast(U16), PASSES)
         acc1 = [psum.tile([P, J], F32, name="acc1_%d" % t) for t in range(PACK)]
+        prod = [tile("prod%d" % z, [P, PACK, J], F32) for z in range(PASSES)]
+        u_bf = [tile("u_bf%d" % z, [P, J, PACK], BF16) for z in range(PASSES)]
+        quantised = [(tile("u_q%d" % z, [P, J], U32), tile("u_s%d" % z, [P, J], U8)) for z in range(PASSES)]
+        j_halves = [(0, J // 2), (J // 2, J)]
+
+        def product(g, parts):
+            z, i = divmod(g, PACK)
+            if g % 2 == 0:
+                first, first_list, second, second_list = xb_sb[g], list_b, xa_whole[g], list_a
+            else:
+                first, first_list, second, second_list = xa_sb[g], list_a, xb_whole[g], list_b
+            picked = tile("picked%d" % g, [P, J], F32)
+            nc.scalar.activation(picked[:], first.indirect(first_list[:]), ACT.Copy)
+            if z == 1:
+                unscaled = picked
+                picked = tile("scaled%d" % g, [P, J], F32)
+                nc.scalar.activation(picked[:], unscaled[:], ACT.Copy, scale=fk_sb[:, z, i : i + 1])
+            for lo, hi in parts:
+                nc.vector.tensor_tensor(
+                    prod[z][:, i, lo:hi], second.indirect(second_list[:, lo // 16 : hi // 16]), picked[:, lo:hi], ALU.mult
+                )
+
+        def quantise_u(z, lo, hi):
+            u_q, u_s = quantised[z]
+            nc.vector.quantize_mx(
+                out=u_q[:, lo:hi].bitcast(E4M3X4),
+                scales=u_s[:, lo:hi],
+                in_=u_bf[z][:, lo:hi, :].rearrange("p j t -> p (j t)"),
+            )
+
+        for g in range(PACK):
+            product(g, [(0, J)])
+            if g == 1:
+                deal(ws_sb[:], ws_raw[:], PASSES)
+        nc.vector.tensor_tensor(
+            u_bf[0][:].rearrange("p (c i) t -> p c t i", i=4),
+            prod[0][:].rearrange("p t (c i) -> p c t i", i=4),
+            fk_sb[:, 0, :].unsqueeze(1).unsqueeze(3).broadcast_to([P, J // 4, PACK, 4]),
+            ALU.mult,
+        )
+        product(4, [(0, J)])
+        quantise_u(0, 0, J)
+        product(5, [(0, J)])
+        product(6, [(0, J)])
+        product(7, j_halves)
+        for lo, hi in j_halves:
+            interleave(nc, u_bf[1][:, lo:hi, :], prod[1][:, :, lo:hi])
+        for lo, hi in j_halves:
+            quantise_u(1, lo, hi)
+
         for z in range(PASSES):
-            prod = tile("prod%d" % z, [P, PACK, J], F32)
-            for i in range(PACK):
-                g = z * PACK + i
-                gb = tile("gb%d" % g, [P, J], F32)
-                window = xb_sb[g // 2][:, (g % 2) * S : (g % 2 + 1) * S]
-                gb_raw = tile("gb_raw%d" % g, [P, J], F32)
-                nc.scalar.activation(gb_raw[:], window.indirect(list_b[:]), ACT.Copy)
-                nc.scalar.activation(gb[:], gb_raw[:], ACT.Copy, scale=fk_sb[:, z, i : i + 1])
-                nc.vector.tensor_tensor(prod[:, i, :], xa_sb[g][:].indirect(list_a[:]), gb[:], ALU.mult)
-                if g == 0:
-                    deal(w_sb[:].bitcast(U16), w_raw[:].bitcast(U16), PASSES)
-                if g == 2:
-                    deal(ws_sb[:], ws_raw[:], PASSES)
-            u_bf = tile("u_bf%d" % z, [P, J, PACK], BF16)
-            u_q = tile("u_q%d" % z, [P, J], U32)
-            u_s = tile("u_s%d" % z, [P, J], U8)
-            interleave(nc, u_bf[:], prod[:])
-            nc.vector.quantize_mx(out=u_q[:].bitcast(E4M3X4), scales=u_s[:], in_=u_bf[:].rearrange("p j t -> p (j t)"))
+            u_q, u_s = quantised[z]
             for t in range(PACK):
                 c = (z * PACK + t) * P
                 nc.tensor.matmul_mx(
@@ -152,17 +194,26 @@ def tile_list_entryproducts_relooked_residual_pl_kernel(
                     stop=(z == PASSES - 1),
                 )
 
-        deal(wbs_sb[:], wbs_raw[:], 1)
+        wb_sb = sb.tile([P, N], I32, name="wb_sb", tag="u_bf1", align_bytes=64)
         deal(wb_sb[:], wb_raw[:], 1)
+        wbs_sb = sb.tile([P, N], U8, name="wbs_sb", tag="scaled7", align_bytes=64)
+        deal(wbs_sb[:], wbs_raw[:], 1)
 
+        halves = [(0, O // 2), (O // 2, O)]
         hid_bf = tile("hid_bf", [P, O, PACK], BF16)
         for t in range(PACK):
             ha = tile("ha%d" % t, [P, J], F32)
             nc.scalar.activation(ha[:], acc1[t][:], ACT.Relu)
-            nc.vector.tensor_copy(hid_bf[:, :, t], ha[:].indirect(list_h[:]))
+            for lo, hi in halves if t == PACK - 1 else [(0, O)]:
+                nc.vector.tensor_copy(hid_bf[:, lo:hi, t], ha[:].indirect(list_h[:, lo // 16 : hi // 16]))
         hid_q = tile("hid_q", [P, O], U32)
         hid_s = tile("hid_s", [P, O], U8)
-        nc.vector.quantize_mx(out=hid_q[:].bitcast(E5M2X4), scales=hid_s[:], in_=hid_bf[:].rearrange("p o t -> p (o t)"))
+        for lo, hi in halves:
+            nc.vector.quantize_mx(
+                out=hid_q[:, lo:hi].bitcast(E5M2X4),
+                scales=hid_s[:, lo:hi],
+                in_=hid_bf[:, lo:hi, :].rearrange("p o t -> p (o t)"),
+            )
 
         y = tile("y", [P, PACK, O], F32)
         for t in range(PACK):
@@ -176,16 +227,28 @@ def tile_list_entryproducts_relooked_residual_pl_kernel(
                 start=True,
                 stop=True,
             )
-            nc.vector.scalar_tensor_tensor(
-                out=y[:, t, :], in0=acc2[:], scalar=gm_sb[:, t : t + 1], in1=rs_sb[:, t, :], op0=ALU.mult, op1=ALU.add
-            )
+            for lo, hi in halves if t == PACK - 1 else [(0, O)]:
+                nc.vector.scalar_tensor_tensor(
+                    out=y[:, t, lo:hi],
+                    in0=acc2[:, lo:hi],
+                    scalar=gm_sb[:, t : t + 1],
+                    in1=rs_sb[:, t, lo:hi],
+                    op0=ALU.mult,
+                    op1=ALU.add,
+                )
         nc.sync.dma_start(out=out_0.rearrange("(p t) o -> p t o", t=PACK), in_=y[:])
 
         y_bf = tile("y_bf", [P, O, PACK], BF16)
         y_q = tile("y_q", [P, O], U32)
         y_s = tile("y_s", [P, O], U8)
-        interleave(nc, y_bf[:], y[:])
-        nc.vector.quantize_mx(out=y_q[:].bitcast(E4M3X4), scales=y_s[:], in_=y_bf[:].rearrange("p o t -> p (o t)"))
+        for lo, hi in halves:
+            interleave(nc, y_bf[:, lo:hi, :], y[:, :, lo:hi])
+        for lo, hi in halves:
+            nc.vector.quantize_mx(
+                out=y_q[:, lo:hi].bitcast(E4M3X4),
+                scales=y_s[:, lo:hi],
+                in_=y_bf[:, lo:hi, :].rearrange("p o t -> p (o t)"),
+            )
         nc.sync.dma_start(out=out_1[0].rearrange("p o t -> p (o t)").bitcast(I32), in_=y_q[:].bitcast(I32))
         for q in range(4):
             queue = nc.sync if q % 2 == 0 else nc.scalar

@@ -59,10 +59,6 @@ def tile_list_entryproducts_relooked_residual_pl_kernel(
         xa_sb = [xa_t[k][:, e * T : (e + 1) * T] for k, gs in enumerate(a_groups) for e in range(len(gs))]
         xb_sb = [xb_t[k][:, e * S : (e + 1) * S] for k, gs in enumerate(b_groups) for e in range(len(gs))]
 
-        warm_in = tile("warm_in", [P, 1], F32)
-        warm_out = tile("warm_out", [P, 1], F32)
-        nc.vector.memset(warm_in[:], 0.0)
-        nc.scalar.activation(warm_out[:], warm_in[:], ACT.Copy)
         nc.vector.memset(ws_raw[:].bitcast(I32), 0)
         nc.vector.memset(wbs_raw[:].bitcast(I32), 0)
 
@@ -78,17 +74,14 @@ def tile_list_entryproducts_relooked_residual_pl_kernel(
         def load_b(k):
             load_planes(xb_t[k], xb, b_groups[k])
 
-        def load_ws(q):
+        def load_ws(r):
             nc.sync.dma_start(
-                out=ws_raw[32 * q : 32 * q + 4, :].bitcast(I32).rearrange("p (z c) -> p z c", z=PASSES),
-                in_=w_scales[:, 4 * q : 4 * q + 4, :].rearrange("z r c -> r z c").bitcast(I32),
+                out=ws_raw[r:P:32, :].bitcast(I32).rearrange("p (z c) -> p z c", z=PASSES),
+                in_=w_scales[:, r:16:4, :].rearrange("z q c -> q z c").bitcast(I32),
             )
 
-        def load_wbs(q):
-            nc.sync.dma_start(
-                out=wbs_raw[32 * q : 32 * q + 4, :].bitcast(I32),
-                in_=wb_scales[0, 4 * q : 4 * q + 4, :].bitcast(I32),
-            )
+        def load_wbs(r):
+            nc.sync.dma_start(out=wbs_raw[r:P:32, :].bitcast(I32), in_=wb_scales[0, r:16:4, :].bitcast(I32))
 
         nc.sync.dma_start(
             out=w_raw[:].bitcast(I32).rearrange("p (z c) -> p z c", z=PASSES),
@@ -99,12 +92,10 @@ def tile_list_entryproducts_relooked_residual_pl_kernel(
         nc.sync.dma_start(out=fk_sb[:], in_=fk.rearrange("(z p i) o -> p z (i o)", p=P, i=PACK))
         nc.sync.dma_start(list_a[:], offs)
         load_a(0)
-        load_ws(0)
         load_b(1)
-        load_ws(1)
-        load_ws(2)
-        load_ws(3)
         load_a(1)
+        for r in range(4):
+            load_ws(r)
         load_b(2)
         load_b(3)
         load_a(2)
@@ -131,7 +122,8 @@ def tile_list_entryproducts_relooked_residual_pl_kernel(
         deal(w_sb[:].bitcast(U16), w_raw[:].bitcast(U16), PASSES)
         acc1 = [psum.tile([P, J], F32, name="acc1_%d" % t) for t in range(PACK)]
         prod = [tile("prod%d" % z, [P, PACK, J], F32) for z in range(PASSES)]
-        u_bf = [tile("u_bf%d" % z, [P, J, PACK], BF16) for z in range(PASSES)]
+        u_bf0 = tile("u_bf0", [P, J, PACK], BF16)
+        u_bf1 = [tile("u_bf1_%d" % h, [P, J // 2, PACK], BF16) for h in range(2)]
         quantised = [(tile("u_q%d" % z, [P, J], U32), tile("u_s%d" % z, [P, J], U8)) for z in range(PASSES)]
         j_halves = [(0, J // 2), (J // 2, J)]
 
@@ -146,39 +138,42 @@ def tile_list_entryproducts_relooked_residual_pl_kernel(
             if z == 1:
                 unscaled = picked
                 picked = tile("scaled%d" % g, [P, J], F32)
-                nc.scalar.activation(picked[:], unscaled[:], ACT.Copy, scale=fk_sb[:, z, i : i + 1])
+                if g == 6:
+                    nc.vector.tensor_scalar(picked[:], unscaled[:], fk_sb[:, z, i : i + 1], None, ALU.mult)
+                else:
+                    nc.scalar.activation(picked[:], unscaled[:], ACT.Copy, scale=fk_sb[:, z, i : i + 1])
             for lo, hi in parts:
                 nc.vector.tensor_tensor(
                     prod[z][:, i, lo:hi], second.indirect(second_list[:, lo // 16 : hi // 16]), picked[:, lo:hi], ALU.mult
                 )
 
-        def quantise_u(z, lo, hi):
+        def quantise_u(z, lo, hi, src):
             u_q, u_s = quantised[z]
             nc.vector.quantize_mx(
                 out=u_q[:, lo:hi].bitcast(E4M3X4),
                 scales=u_s[:, lo:hi],
-                in_=u_bf[z][:, lo:hi, :].rearrange("p j t -> p (j t)"),
+                in_=src[:].rearrange("p j t -> p (j t)"),
             )
 
         for g in range(PACK):
             product(g, [(0, J)])
-            if g == 1:
+            if g == 2:
                 deal(ws_sb[:], ws_raw[:], PASSES)
         nc.vector.tensor_tensor(
-            u_bf[0][:].rearrange("p (c i) t -> p c t i", i=4),
+            u_bf0[:].rearrange("p (c i) t -> p c t i", i=4),
             prod[0][:].rearrange("p t (c i) -> p c t i", i=4),
             fk_sb[:, 0, :].unsqueeze(1).unsqueeze(3).broadcast_to([P, J // 4, PACK, 4]),
             ALU.mult,
         )
         product(4, [(0, J)])
-        quantise_u(0, 0, J)
+        quantise_u(0, 0, J, u_bf0)
         product(5, [(0, J)])
         product(6, [(0, J)])
         product(7, j_halves)
-        for lo, hi in j_halves:
-            interleave(nc, u_bf[1][:, lo:hi, :], prod[1][:, :, lo:hi])
-        for lo, hi in j_halves:
-            quantise_u(1, lo, hi)
+        for h, (lo, hi) in enumerate(j_halves):
+            interleave(nc, u_bf1[h][:], prod[1][:, :, lo:hi])
+        for h, (lo, hi) in enumerate(j_halves):
+            quantise_u(1, lo, hi, u_bf1[h])
 
         for z in range(PASSES):
             u_q, u_s = quantised[z]
@@ -194,9 +189,12 @@ def tile_list_entryproducts_relooked_residual_pl_kernel(
                     stop=(z == PASSES - 1),
                 )
 
-        wb_sb = sb.tile([P, N], I32, name="wb_sb", tag="u_bf1", align_bytes=64)
-        deal(wb_sb[:], wb_raw[:], 1)
-        wbs_sb = sb.tile([P, N], U8, name="wbs_sb", tag="scaled7", align_bytes=64)
+        wb_sb = sb.tile([P, N], I32, name="wb_sb", tag="u_bf1_1", align_bytes=64)
+        nc.vector.tensor_copy(
+            out=wb_sb[:].rearrange("p (t c i) -> p c t i", t=PACK, i=4),
+            in_=wb_raw[:].rearrange("p (c i t) -> p c t i", t=PACK, i=4),
+        )
+        wbs_sb = sb.tile([P, N], U8, name="wbs_sb", tag="u_bf1_0", align_bytes=64)
         deal(wbs_sb[:], wbs_raw[:], 1)
 
         halves = [(0, O // 2), (O // 2, O)]
@@ -253,5 +251,5 @@ def tile_list_entryproducts_relooked_residual_pl_kernel(
         for q in range(4):
             queue = nc.sync if q % 2 == 0 else nc.scalar
             queue.dma_start(
-                out=out_2[0, 4 * q : 4 * q + 4, :].bitcast(I32), in_=y_s[32 * q : 32 * q + 4, :].bitcast(I32)
+                out=out_2[0, q:16:4, :].bitcast(I32), in_=y_s[q:P:32, :].bitcast(I32)
             )

@@ -50,15 +50,16 @@ def tile_list_entryproducts_relooked_residual_pl_kernel(
         ws_raw = tile("ws_raw", [P, PASSES * R], U8)
         wb_raw = tile("wb_raw", [P, N], I32)
         wbs_raw = tile("wbs_raw", [P, N], U8)
-        a_groups = [(0, 1), (2, 3), (4, 5), (6,), (7,)]
-        b_groups = [(0,), (1, 2), (3,), (4,), (5, 6), (7,)]
-        xa_t = [tile("xa%d" % gs[0], [P, len(gs) * T], F32) for gs in a_groups]
-        xb_t = [tile("xb%d" % gs[0], [P, len(gs) * S], F32) for gs in b_groups]
-        xa_whole = {gs[0]: xa_t[k][:] for k, gs in enumerate(a_groups)}
-        xb_whole = {gs[0]: xb_t[k][:] for k, gs in enumerate(b_groups)}
-        xa_sb = [xa_t[k][:, e * T : (e + 1) * T] for k, gs in enumerate(a_groups) for e in range(len(gs))]
-        xb_sb = [xb_t[k][:, e * S : (e + 1) * S] for k, gs in enumerate(b_groups) for e in range(len(gs))]
+        groups = [(0, 1), (2, 3), (4, 5), (6,), (7,)]
+        xa_t = [tile("xa%d" % gs[0], [P, len(gs) * T], F32) for gs in groups]
+        xb_t = [tile("xb%d" % gs[0], [P, len(gs) * S], F32) for gs in groups]
+        xa_sb = [xa_t[k][:, e * T : (e + 1) * T] for k, gs in enumerate(groups) for e in range(len(gs))]
+        xb_sb = [xb_t[k][:, e * S : (e + 1) * S] for k, gs in enumerate(groups) for e in range(len(gs))]
 
+        warm_in = tile("warm_in", [P, 1], F32)
+        warm_out = tile("warm_out", [P, 1], F32)
+        nc.vector.memset(warm_in[:], 0.0)
+        nc.scalar.activation(warm_out[:], warm_in[:], ACT.Copy)
         nc.vector.memset(ws_raw[:].bitcast(I32), 0)
         nc.vector.memset(wbs_raw[:].bitcast(I32), 0)
 
@@ -69,10 +70,10 @@ def tile_list_entryproducts_relooked_residual_pl_kernel(
             nc.sync.dma_start(out=dst[:], in_=rows[gs[0] // PACK, :, i * width : (i + len(gs)) * width])
 
         def load_a(k):
-            load_planes(xa_t[k], xa, a_groups[k])
+            load_planes(xa_t[k], xa, groups[k])
 
         def load_b(k):
-            load_planes(xb_t[k], xb, b_groups[k])
+            load_planes(xb_t[k], xb, groups[k])
 
         def load_ws(r):
             nc.sync.dma_start(
@@ -93,16 +94,12 @@ def tile_list_entryproducts_relooked_residual_pl_kernel(
         nc.sync.dma_start(list_a[:], offs)
         load_a(0)
         load_b(1)
-        load_a(1)
         for r in range(4):
             load_ws(r)
-        load_b(2)
-        load_b(3)
-        load_a(2)
-        load_b(4)
-        load_a(4)
-        load_a(3)
-        load_b(5)
+        load_a(1)
+        for k in range(2, len(groups)):
+            load_b(k)
+            load_a(k)
         nc.sync.dma_start(out=wb_raw[:], in_=wb_words[0].rearrange("p n t -> p (n t)").bitcast(I32))
         for q in range(4):
             load_wbs(q)
@@ -127,24 +124,28 @@ def tile_list_entryproducts_relooked_residual_pl_kernel(
         quantised = [(tile("u_q%d" % z, [P, J], U32), tile("u_s%d" % z, [P, J], U8)) for z in range(PASSES)]
         j_halves = [(0, J // 2), (J // 2, J)]
 
+        def gather(on_vector, dst, window, offsets):
+            if on_vector:
+                nc.vector.tensor_copy(dst, window.indirect(offsets))
+            else:
+                nc.scalar.activation(dst, window.indirect(offsets), ACT.Copy)
+
         def product(g, parts):
             z, i = divmod(g, PACK)
-            if g % 2 == 0:
-                first, first_list, second, second_list = xb_sb[g], list_b, xa_whole[g], list_a
-            else:
-                first, first_list, second, second_list = xa_sb[g], list_a, xb_whole[g], list_b
-            picked = tile("picked%d" % g, [P, J], F32)
-            nc.scalar.activation(picked[:], first.indirect(first_list[:]), ACT.Copy)
-            if z == 1:
-                unscaled = picked
-                picked = tile("scaled%d" % g, [P, J], F32)
-                if g == 6:
-                    nc.vector.tensor_scalar(picked[:], unscaled[:], fk_sb[:, z, i : i + 1], None, ALU.mult)
-                else:
-                    nc.scalar.activation(picked[:], unscaled[:], ACT.Copy, scale=fk_sb[:, z, i : i + 1])
-            for lo, hi in parts:
-                nc.vector.tensor_tensor(
-                    prod[z][:, i, lo:hi], second.indirect(second_list[:, lo // 16 : hi // 16]), picked[:, lo:hi], ALU.mult
+            gb = tile("gb%d" % g, [P, J], F32)
+            gather(False, gb[:], xb_sb[g], list_b[:])
+            ga = [tile("ga%d_%d" % (g, lo), [P, hi - lo], F32) for lo, hi in parts]
+            for h, (lo, hi) in enumerate(parts):
+                on_vector = g % 2 == 0 or (g == 7 and h == 0)
+                gather(on_vector, ga[h][:], xa_sb[g], list_a[:, lo // 16 : hi // 16])
+            for h, (lo, hi) in enumerate(parts):
+                nc.vector.scalar_tensor_tensor(
+                    out=prod[z][:, i, lo:hi],
+                    in0=ga[h][:],
+                    scalar=fk_sb[:, z, i : i + 1],
+                    in1=gb[:, lo:hi],
+                    op0=ALU.mult,
+                    op1=ALU.mult,
                 )
 
         def quantise_u(z, lo, hi, src):
@@ -157,14 +158,9 @@ def tile_list_entryproducts_relooked_residual_pl_kernel(
 
         for g in range(PACK):
             product(g, [(0, J)])
-            if g == 2:
+            if g == 1:
                 deal(ws_sb[:], ws_raw[:], PASSES)
-        nc.vector.tensor_tensor(
-            u_bf0[:].rearrange("p (c i) t -> p c t i", i=4),
-            prod[0][:].rearrange("p t (c i) -> p c t i", i=4),
-            fk_sb[:, 0, :].unsqueeze(1).unsqueeze(3).broadcast_to([P, J // 4, PACK, 4]),
-            ALU.mult,
-        )
+        interleave(nc, u_bf0[:], prod[0][:])
         product(4, [(0, J)])
         quantise_u(0, 0, J, u_bf0)
         product(5, [(0, J)])

from contextlib import ExitStack

import concourse.mybir as mybir

K, T, J, S, R, O, N = 1024, 512, 256, 512, 512, 128, 512
FLOPS = 2 * K * R * J + 2 * R * N * O

F32 = mybir.dt.float32
BF16 = mybir.dt.bfloat16
I32 = mybir.dt.int32
U32 = mybir.dt.uint32
U16 = mybir.dt.uint16
U8 = mybir.dt.uint8
E4M3X4 = mybir.dt.float8_e4m3fn_x4
E5M2X4 = mybir.dt.float8_e5m2_x4
E2M1X4 = mybir.dt.float4_e2m1fn_x4
ALU = mybir.AluOpType
ACT = mybir.ActivationFunctionType

P = 128
PACK = 4
PASSES = K // (P * PACK)


def interleave(nc, dst, src):
    nc.vector.tensor_copy(
        out=dst.rearrange("p (c i) t -> p c t i", i=4),
        in_=src.rearrange("p t (c i) -> p c t i", i=4),
    )


def tile_list_entryproducts_relooked_residual_pl_kernel(
    tc, xa, xb, fk, w_words, w_scales, wb_words, wb_scales, rs, gm, offs, offs2, offs3, out_0, out_1, out_2
):
    nc = tc.nc
    with ExitStack() as ctx:
        sb = ctx.enter_context(tc.tile_pool(name="sb", bufs=1))
        psum = ctx.enter_context(tc.psum_pool(name="psum", bufs=1))

        def tile(name, shape, dtype):
            return sb.tile(shape, dtype, name=name, align_bytes=64)

        list_a = tile("list_a", [P, J // 16], U16)
        list_b = tile("list_b", [P, J // 16], U16)
        list_h = tile("list_h", [P, O // 16], U16)
        fk_sb = tile("fk_sb", [P, PASSES, PACK], F32)
        gm_sb = tile("gm_sb", [P, PACK], F32)
        rs_sb = tile("rs_sb", [P, PACK, O], F32)
        w_raw = tile("w_raw", [P, PASSES * 2 * R], U8)
        ws_raw = tile("ws_raw", [P, PASSES * R], U8)
        wb_raw = tile("wb_raw", [P, N], I32)
        wbs_raw = tile("wbs_raw", [P, N], U8)
        groups = [(0, 1), (2, 3), (4, 5), (6,), (7,)]
        xa_t = [tile("xa%d" % gs[0], [P, len(gs) * T], F32) for gs in groups]
        xb_t = [tile("xb%d" % gs[0], [P, len(gs) * S], F32) for gs in groups]
        xa_sb = [xa_t[k][:, e * T : (e + 1) * T] for k, gs in enumerate(groups) for e in range(len(gs))]
        xb_sb = [xb_t[k][:, e * S : (e + 1) * S] for k, gs in enumerate(groups) for e in range(len(gs))]

        warm_in = tile("warm_in", [P, 1], F32)
        warm_out = tile("warm_out", [P, 1], F32)
        nc.vector.memset(warm_in[:], 0.0)
        nc.scalar.activation(warm_out[:], warm_in[:], ACT.Copy)
        nc.vector.memset(ws_raw[:].bitcast(I32), 0)
        nc.vector.memset(wbs_raw[:].bitcast(I32), 0)

        def load_planes(dst, table, gs):
            rows = table.rearrange("(z p i) c -> z p (i c)", p=P, i=PACK)
            width = table.shape[1]
            i = gs[0] % PACK
            nc.sync.dma_start(out=dst[:], in_=rows[gs[0] // PACK, :, i * width : (i + len(gs)) * width])

        def load_a(k):
            load_planes(xa_t[k], xa, groups[k])

        def load_b(k):
            load_planes(xb_t[k], xb, groups[k])

        def load_ws(r):
            nc.sync.dma_start(
                out=ws_raw[r:P:32, :].bitcast(I32).rearrange("p (z c) -> p z c", z=PASSES),
                in_=w_scales[:, r:16:4, :].rearrange("z q c -> q z c").bitcast(I32),
            )

        def load_wbs(r):
            nc.sync.dma_start(out=wbs_raw[r:P:32, :].bitcast(I32), in_=wb_scales[0, r:16:4, :].bitcast(I32))

        nc.sync.dma_start(
            out=w_raw[:].bitcast(I32).rearrange("p (z c) -> p z c", z=PASSES),
            in_=w_words.rearrange("z p c -> p z c").bitcast(I32),
        )
        nc.sync.dma_start(list_b[:], offs2)
        load_b(0)
        nc.sync.dma_start(out=fk_sb[:], in_=fk.rearrange("(z p i) o -> p z (i o)", p=P, i=PACK))
        nc.sync.dma_start(list_a[:], offs)
        load_a(0)
        load_b(1)
        for r in range(4):
            load_ws(r)
        load_a(1)
        for k in range(2, len(groups)):
            load_b(k)
            load_a(k)
        nc.sync.dma_start(out=wb_raw[:], in_=wb_words[0].rearrange("p n t -> p (n t)").bitcast(I32))
        for q in range(4):
            load_wbs(q)
        nc.sync.dma_start(list_h[:], offs3)
        nc.sync.dma_start(out=gm_sb[:], in_=gm.rearrange("(p t) o -> p (t o)", t=PACK))
        nc.sync.dma_start(out=rs_sb[:], in_=rs.rearrange("(p t) o -> p t o", t=PACK))

        w_sb = tile("w_sb", [P, PASSES * 2 * R], U8)
        ws_sb = tile("ws_sb", [P, PASSES * R], U8)

        def deal(dst, src, z):
            nc.vector.tensor_copy(
                out=dst.rearrange("p (z t m) -> p z t m", z=z, t=PACK),
                in_=src.rearrange("p (z m t) -> p z t m", z=z, t=PACK),
            )

        deal(w_sb[:].bitcast(U16), w_raw[:].bitcast(U16), PASSES)
        acc1 = [psum.tile([P, J], F32, name="acc1_%d" % t) for t in range(PACK)]
        prod = [tile("prod%d" % z, [P, PACK, J], F32) for z in range(PASSES)]
        u_bf0 = tile("u_bf0", [P, J, PACK], BF16)
        u_bf1 = [tile("u_bf1_%d" % h, [P, J // 2, PACK], BF16) for h in range(2)]
        quantised = [(tile("u_q%d" % z, [P, J], U32), tile("u_s%d" % z, [P, J], U8)) for z in range(PASSES)]
        j_halves = [(0, J // 2), (J // 2, J)]

        def gather(on_vector, dst, window, offsets):
            if on_vector:
                nc.vector.tensor_copy(dst, window.indirect(offsets))
            else:
                nc.scalar.activation(dst, window.indirect(offsets), ACT.Copy)

        def product(g, parts):
            z, i = divmod(g, PACK)
            gb = tile("gb%d" % g, [P, J], F32)
            gather(False, gb[:], xb_sb[g], list_b[:])
            ga = [tile("ga%d_%d" % (g, lo), [P, hi - lo], F32) for lo, hi in parts]
            for h, (lo, hi) in enumerate(parts):
                on_vector = g % 2 == 0 or (g == 7 and h == 0)
                gather(on_vector, ga[h][:], xa_sb[g], list_a[:, lo // 16 : hi // 16])
            for h, (lo, hi) in enumerate(parts):
                nc.vector.scalar_tensor_tensor(
                    out=prod[z][:, i, lo:hi],
                    in0=ga[h][:],
                    scalar=fk_sb[:, z, i : i + 1],
                    in1=gb[:, lo:hi],
                    op0=ALU.mult,
                    op1=ALU.mult,
                )

        def quantise_u(z, lo, hi, src):
            u_q, u_s = quantised[z]
            nc.vector.quantize_mx(
                out=u_q[:, lo:hi].bitcast(E4M3X4),
                scales=u_s[:, lo:hi],
                in_=src[:].rearrange("p j t -> p (j t)"),
            )

        for g in range(PACK):
            product(g, [(0, J)])
            if g == 1:
                deal(ws_sb[:], ws_raw[:], PASSES)
        interleave(nc, u_bf0[:], prod[0][:])
        product(4, [(0, J)])
        quantise_u(0, 0, J, u_bf0)
        product(5, [(0, J)])
        product(6, [(0, J)])
        product(7, j_halves)
        for h, (lo, hi) in enumerate(j_halves):
            interleave(nc, u_bf1[h][:], prod[1][:, :, lo:hi])
        for h, (lo, hi) in enumerate(j_halves):
            quantise_u(1, lo, hi, u_bf1[h])

        for z in range(PASSES):
            u_q, u_s = quantised[z]
            for t in range(PACK):
                c = (z * PACK + t) * P
                nc.tensor.matmul_mx(
                    out=acc1[t][:],
                    lhsT=w_sb[:, 2 * c : 2 * (c + P)].bitcast(E2M1X4),
                    lhsT_scale=ws_sb[:, c : c + P],
                    rhs=u_q[:].bitcast(E4M3X4),
                    rhs_scale=u_s[:],
                    start=(z == 0),
                    stop=(z == PASSES - 1),
                )

        wb_sb = sb.tile([P, N], I32, name="wb_sb", tag="u_bf1_1", align_bytes=64)
        nc.vector.tensor_copy(
            out=wb_sb[:].rearrange("p (t c i) -> p c t i", t=PACK, i=4),
            in_=wb_raw[:].rearrange("p (c i t) -> p c t i", t=PACK, i=4),
        )
        wbs_sb = sb.tile([P, N], U8, name="wbs_sb", tag="u_bf1_0", align_bytes=64)
        deal(wbs_sb[:], wbs_raw[:], 1)

        halves = [(0, O // 2), (O // 2, O)]
        hid_bf = tile("hid_bf", [P, O, PACK], BF16)
        for t in range(PACK):
            ha = tile("ha%d" % t, [P, J], F32)
            nc.scalar.activation(ha[:], acc1[t][:], ACT.Relu)
            for lo, hi in halves if t == PACK - 1 else [(0, O)]:
                nc.vector.tensor_copy(hid_bf[:, lo:hi, t], ha[:].indirect(list_h[:, lo // 16 : hi // 16]))
        hid_q = tile("hid_q", [P, O], U32)
        hid_s = tile("hid_s", [P, O], U8)
        for lo, hi in halves:
            nc.vector.quantize_mx(
                out=hid_q[:, lo:hi].bitcast(E5M2X4),
                scales=hid_s[:, lo:hi],
                in_=hid_bf[:, lo:hi, :].rearrange("p o t -> p (o t)"),
            )

        y = tile("y", [P, PACK, O], F32)
        for t in range(PACK):
            acc2 = psum.tile([P, O], F32, name="acc2_%d" % t)
            nc.tensor.matmul_mx(
                out=acc2[:],
                lhsT=wb_sb[:, t * P : (t + 1) * P].bitcast(E5M2X4),
                lhsT_scale=wbs_sb[:, t * P : (t + 1) * P],
                rhs=hid_q[:].bitcast(E5M2X4),
                rhs_scale=hid_s[:],
                start=True,
                stop=True,
            )
            for lo, hi in halves if t == PACK - 1 else [(0, O)]:
                nc.vector.scalar_tensor_tensor(
                    out=y[:, t, lo:hi],
                    in0=acc2[:, lo:hi],
                    scalar=gm_sb[:, t : t + 1],
                    in1=rs_sb[:, t, lo:hi],
                    op0=ALU.mult,
                    op1=ALU.add,
                )
        nc.sync.dma_start(out=out_0.rearrange("(p t) o -> p t o", t=PACK), in_=y[:])

        y_bf = tile("y_bf", [P, O, PACK], BF16)
        y_q = tile("y_q", [P, O], U32)
        y_s = tile("y_s", [P, O], U8)
        for lo, hi in halves:
            interleave(nc, y_bf[:, lo:hi, :], y[:, :, lo:hi])
        for lo, hi in halves:
            nc.vector.quantize_mx(
                out=y_q[:, lo:hi].bitcast(E4M3X4),
                scales=y_s[:, lo:hi],
                in_=y_bf[:, lo:hi, :].rearrange("p o t -> p (o t)"),
            )
        nc.sync.dma_start(out=out_1[0].rearrange("p o t -> p (o t)").bitcast(I32), in_=y_q[:].bitcast(I32))
        for q in range(4):
            queue = nc.sync if q % 2 == 0 else nc.scalar
            queue.dma_start(
                out=out_2[0, q:16:4, :].bitcast(I32), in_=y_s[q:P:32, :].bitcast(I32)
            )
